import numpy as np
import ml_dtypes


def mxq(x, axis, fmt="e4m3"):
    dtype, down = {"e4m3": (ml_dtypes.float8_e4m3fn, 7), "e5m2": (ml_dtypes.float8_e5m2, 14)}[fmt]
    v = np.moveaxis(np.asarray(x, np.float32).astype(ml_dtypes.bfloat16).astype(np.float64), axis, -1)
    blocks = v.reshape(v.shape[:-1] + (-1, 32))
    amax = np.abs(blocks).max(-1, keepdims=True)
    byte = np.maximum(np.where(amax > 0, np.frexp(amax)[1] - 1 + 127, 0) - down, 1)
    scale = np.exp2(byte - 127.0)
    codes = (blocks / scale).astype(np.float32).astype(dtype).astype(np.float64)
    return np.moveaxis((codes * scale).reshape(v.shape), -1, axis)


WIDE = False


def mx_kscale(k):
    if not WIDE:
        return np.ones(k)
    levels = np.array([10, -10, 5, -5, 0])
    if k % 512:
        return np.exp2(np.random.permutation(np.resize(levels, k // 32))).repeat(32)
    a = np.empty((k // 512, 16))
    for p in range(k // 512):
        a[p, :8] = np.random.permutation(np.resize(levels, 8))
        for g in range(8):
            far = levels[np.abs(levels - a[p, g]) >= 10]
            a[p, g + 8] = far[np.random.randint(len(far))]
    return np.exp2(a.ravel()).repeat(32)


def f64(x):
    return np.asarray(x).astype(np.float64)


def striped(idx):
    return np.tile(idx.reshape(-1, 16).T, (8, 1)).astype(np.uint16)


def unstriped(offs):
    return offs[:16].T.reshape(-1).astype(np.int64)


def striped8(idx):
    return np.concatenate([x.reshape(-1, 16).T for x in idx]).astype(np.uint16)


def runs(offs, k):
    lists = np.stack([offs[16 * r : 16 * r + 16].T.reshape(-1) for r in range(8)]).astype(np.int64)
    return lists[np.arange(k) % 512 // 64]


def pack_weight(w):
    k, n = w.shape
    w = f64(np.asarray(w, np.float32).astype(ml_dtypes.bfloat16)).reshape(k // 32, 32, n)
    amax = np.abs(w).max(1)
    byte = np.clip(np.where(amax > 0, np.frexp(amax)[1] - 1 + 127 - 7, 1), 1, 254)
    scaled = (w * np.exp2(127.0 - byte)[:, None, :]).reshape(k, n).astype(np.float32)
    words = np.ascontiguousarray(scaled.reshape(k // 512, 128, 4, n).transpose(0, 1, 3, 2)).astype(ml_dtypes.float8_e4m3fn).view(np.uint8)
    return words, np.ascontiguousarray(byte.astype(np.uint8).reshape(k // 512, 16, n))


def unpack_weight(words, scales):
    g, p, n, _ = words.shape
    vals = np.ascontiguousarray(words).view(ml_dtypes.float8_e4m3fn).astype(np.float64) * np.repeat(np.exp2(scales.astype(np.float64) - 127.0), 8, axis=1)[..., None]
    return vals.transpose(0, 1, 3, 2).reshape(g * 512, n)


K, T, S, G, H, W = 512, 1024, 256, 2048, 512, 128


def setup_inputs():
    n = np.random.standard_normal
    s = mx_kscale(K)[:, None]
    packed_xT = pack_weight(n((K, T)) * s)
    packed_dT = pack_weight(n((K, G)) / s)
    perm = np.random.permutation(S)
    perm2 = np.random.permutation(S)
    perm3 = np.random.permutation(S)
    return {
        "x_words": packed_xT[0],
        "x_scales": packed_xT[1],
        "d_words": packed_dT[0],
        "d_scales": packed_dT[1],
        "gs": (np.random.uniform(0.5, 1.5, (K, 1)) * s).astype(np.float32),
        "offs": striped8(np.random.randint(0, T, (8, S))),
        "k1": striped8(np.random.randint(0, G, (8, H))),
        "hz": striped8(np.random.randint(0, T, (8, S))),
        "k2": striped8(np.random.randint(0, G, (8, H))),
        "n1": striped(perm[:W]),
        "n2": striped(perm[W:]),
        "k3": striped8(np.random.randint(0, G, (8, H))),
        "k4": striped8(np.random.randint(0, G, (8, H))),
        "hy": striped8(np.random.randint(0, T, (8, S))),
        "n3": striped(perm2[:W]),
        "n4": striped(perm2[W:]),
        "n5": striped(perm3[:W]),
        "n6": striped(perm3[W:]),
        "n7": striped(np.random.permutation(S)),
    }


def reference(x_words, x_scales, d_words, d_scales, gs, offs, k1, hz, k2, n1, n2, k3, k4, hy, n3, n4, n5, n6, n7):
    d_k3 = unpack_weight(d_words, d_scales)[np.arange(K)[:, None], runs(k3, K)]
    d_k1 = unpack_weight(d_words, d_scales)[np.arange(K)[:, None], runs(k1, K)]
    xq = unpack_weight(x_words, x_scales)[np.arange(K)[:, None], runs(offs, K)]
    d_k2 = unpack_weight(d_words, d_scales)[np.arange(K)[:, None], runs(k2, K)]
    x_hz = unpack_weight(x_words, x_scales)[np.arange(K)[:, None], runs(hz, K)]
    h = 0.0625 * (d_k1.T @ xq + d_k2.T @ x_hz)
    pb = h[:, unstriped(n2)]
    pa = h[:, unstriped(n1)]
    rb = pb - (0.5 * pa)
    ra = np.sqrt((pa) ** 2 + (pb) ** 2 + 0.25)
    ua = np.zeros((H, S))
    ua[:, unstriped(n1)] = ra
    ub = ua.copy()
    ub[:, unstriped(n2)] = rb
    z = f64(gs) * ub
    d_k4 = unpack_weight(d_words, d_scales)[np.arange(K)[:, None], runs(k4, K)]
    x_hy = unpack_weight(x_words, x_scales)[np.arange(K)[:, None], runs(hy, K)]
    h2 = 0.0625 * ((d_k3.T @ mxq(z, 0, "e4m3") + d_k4.T @ x_hy))
    pa2 = h2[:, unstriped(n3)]
    pb2 = h2[:, unstriped(n4)]
    ra2 = pb2 - pa2
    ua2 = np.zeros((H, S))
    ua2[:, unstriped(n5)] = ra2
    ub2 = ua2.copy()
    ub2[:, unstriped(n6)] = pa2
    return np.maximum(ub2, h2[:, unstriped(n7)])

@@ -1,0 +1,213 @@
+from contextlib import ExitStack
+
+import concourse.mybir as mybir
+
+K, T, S, G, H, W = 512, 1024, 256, 2048, 512, 128
+P = 128
+FLOPS = 4 * 2 * K * H * S
+
+F32, BF16 = mybir.dt.float32, mybir.dt.bfloat16
+I32, U32, U16, U8 = mybir.dt.int32, mybir.dt.uint32, mybir.dt.uint16, mybir.dt.uint8
+FP8X4 = mybir.dt.float8_e4m3fn_x4
+ALU = mybir.AluOpType
+ACT = mybir.ActivationFunctionType
+
+
+def tile_picked_mhhzmhpolarcphw_none_p_kernel(
+    tc, x_words, x_scales, d_words, d_scales, gs, offs, k1, hz, k2, n1, n2, k3, k4, hy, n3, n4, n5, n6, n7, out
+):
+    nc = tc.nc
+    with ExitStack() as ctx:
+        sb = ctx.enter_context(tc.tile_pool(name="sb", bufs=1))
+        psum = ctx.enter_context(tc.psum_pool(name="psum", bufs=1))
+
+        def tile(name, shape, dtype):
+            return sb.tile(shape, dtype, name=name, align_bytes=64)
+
+        def load_list(name, src):
+            t = tile(name, list(src.shape), U16)
+            nc.sync.dma_start(t[:], src)
+            return t
+
+        def load_scale_table(name, src, cols):
+            t = tile(name, [P, cols], U8)
+            rows = src[0].bitcast(I32).unsqueeze(1).broadcast_to([16, 8, cols // 4])
+            nc.sync.dma_start(t[:].bitcast(I32), rows)
+            return t
+
+        def load_word_table(name, src, cols):
+            t = tile(name, [P, cols], I32)
+            nc.sync.dma_start(t[:], src[0].rearrange("p n t -> p (n t)").bitcast(I32))
+            return t
+
+        x_sc = load_scale_table("x_sc", x_scales, T)
+        l_offs = load_list("l_offs", offs)
+        d_sc = load_scale_table("d_sc", d_scales, G)
+        l_hz = load_list("l_hz", hz)
+        l_k1 = load_list("l_k1", k1)
+        l_k2 = load_list("l_k2", k2)
+        x_w = load_word_table("x_w", x_words, T)
+        d_w = load_word_table("d_w", d_words, G)
+        l_n1 = load_list("l_n1", n1)
+        l_n2 = load_list("l_n2", n2)
+        gs_t = tile("gs_t", [P, 4], F32)
+        nc.sync.dma_start(gs_t[:], gs.rearrange("(p t) o -> p (t o)", t=4))
+        l_hy = load_list("l_hy", hy)
+        l_k4 = load_list("l_k4", k4)
+        l_k3 = load_list("l_k3", k3)
+        l_n3 = load_list("l_n3", n3)
+        l_n4 = load_list("l_n4", n4)
+        l_n7 = load_list("l_n7", n7)
+        l_n6 = load_list("l_n6", n6)
+        l_n5 = load_list("l_n5", n5)
+
+        def gather_bytes(dst, table, lst):
+            nc.vector.tensor_copy(dst, table[:].indirect(lst))
+
+        def gather_words(dst, table, lst):
+            nc.vector.tensor_copy(dst, table[:].bitcast(U32).indirect(lst))
+
+        def place_scale_rows(name, picked, cols, queue):
+            placed = tile(name, [P, cols], U8)
+            nc.gpsimd.memset(placed[:].bitcast(I32), 0)
+            for i in range(4):
+                queue.dma_start(placed[i:P:32, :].bitcast(I32), picked[8 * i : P : 32, :].bitcast(I32))
+            return placed
+
+        picked1 = tile("picked1", [P, 2 * S + 2 * H], U8)
+        gather_bytes(picked1[:, 0:S], x_sc, l_offs[:])
+        gather_bytes(picked1[:, S : 2 * S], x_sc, l_hz[:])
+        gather_bytes(picked1[:, 2 * S : 2 * S + H], d_sc, l_k1[:])
+        gather_bytes(picked1[:, 2 * S + H :], d_sc, l_k2[:])
+        placed1 = place_scale_rows("placed1", picked1, 2 * S + 2 * H, nc.scalar)
+
+        xq_w = tile("xq_w", [P, S], U32)
+        xz_w = tile("xz_w", [P, S], U32)
+        d12_w = tile("d12_w", [P, 2 * H], U32)
+        gather_words(xq_w[:], x_w, l_offs[:])
+        gather_words(xz_w[:], x_w, l_hz[:])
+        gather_words(d12_w[:, 0:H], d_w, l_k1[:])
+        gather_words(d12_w[:, H:], d_w, l_k2[:])
+
+        h_sb = []
+        for t in range(4):
+            dw = tile("dealt_w%d" % t, [P, 2 * P], I32)
+            ds = tile("dealt_s%d" % t, [P, 2 * P], U8)
+            nc.vector.tensor_copy(dw[:], d12_w[:, t : 2 * H : 4].bitcast(I32))
+            nc.vector.tensor_copy(ds[:], placed1[:, 2 * S + t : 2 * S + 2 * H : 4])
+            acc = psum.tile([P, S], F32, name="h_ps%d" % t)
+            for j, xw in enumerate((xq_w, xz_w)):
+                nc.tensor.matmul_mx(
+                    out=acc[:],
+                    lhsT=dw[:, j * P : (j + 1) * P].bitcast(FP8X4),
+                    lhsT_scale=ds[:, j * P : (j + 1) * P],
+                    rhs=xw[:].bitcast(FP8X4),
+                    rhs_scale=placed1[:, j * S : (j + 1) * S],
+                    start=(j == 0),
+                    stop=(j == 1),
+                )
+            h = tile("h%d" % t, [P, S], F32)
+            if t == 0:
+                nc.scalar.activation(h[:], acc[:], ACT.Copy, scale=0.0625)
+            else:
+                nc.vector.tensor_scalar(h[:], acc[:], 0.0625, None, ALU.mult)
+            h_sb.append(h)
+
+        pab = [tile("pab%d" % u, [P, 2, 2 * W], F32) for u in range(2)]
+        for t in range(4):
+            nc.scalar.activation(pab[t // 2][:, t % 2, 0:W], h_sb[t][:].indirect(l_n1[:]), ACT.Copy)
+            nc.scalar.activation(pab[t // 2][:, t % 2, W:], h_sb[t][:].indirect(l_n2[:]), ACT.Copy)
+        rb = [tile("rb%d" % u, [P, 2, W], F32) for u in range(2)]
+        ssq = tile("ssq", [P, 4 * W], F32)
+        ra = tile("ra", [P, 4 * W], F32)
+        for u in range(2):
+            nc.vector.scalar_tensor_tensor(rb[u][:], pab[u][:, :, 0:W], -0.5, pab[u][:, :, W:], ALU.mult, ALU.add)
+        for u in range(2):
+            sq = sb.tile([P, 2, 2 * W], F32, name="sq%d" % u, tag="scratch%d" % u, align_bytes=64)
+            nc.vector.tensor_tensor(sq[:], pab[u][:], pab[u][:], ALU.mult)
+            nc.vector.scalar_tensor_tensor(
+                ssq[:, 2 * u * W : 2 * (u + 1) * W].rearrange("p (t w) -> p t w", t=2),
+                sq[:, :, 0:W], 0.25, sq[:, :, W:], ALU.add, ALU.add,
+            )
+        ub = [tile("ub%d" % t, [P, S], F32) for t in range(4)]
+        for t in range(4):
+            nc.scalar.activation(ub[t][:].indirect(l_n2[:]), rb[t // 2][:, t % 2, :], ACT.Copy)
+        nc.scalar.activation(ra[:], ssq[:], ACT.Sqrt)
+        for t in range(4):
+            nc.scalar.activation(ub[t][:].indirect(l_n1[:]), ra[:, t * W : (t + 1) * W], ACT.Copy)
+
+        picked2 = sb.tile([P, S + 2 * H], U8, name="picked2", tag="scratch1", align_bytes=64)
+        gather_bytes(picked2[:, 0:S], x_sc, l_hy[:])
+        gather_bytes(picked2[:, S : S + H], d_sc, l_k4[:])
+        gather_bytes(picked2[:, S + H :], d_sc, l_k3[:])
+        placed2 = place_scale_rows("placed2", picked2, S + 2 * H, nc.sync)
+        HH = H // 2
+        early_w = sb.tile([P, S + H], U32, name="early_w", tag="scratch0", align_bytes=64)
+        gather_words(early_w[:, 0:S], x_w, l_hy[:])
+        gather_words(early_w[:, S : S + HH], d_w, l_k4[:, 0:16])
+        gather_words(early_w[:, S + HH :], d_w, l_k3[:, 0:16])
+
+        z_bf = sb.tile([P, S, 4], BF16, name="z_bf", tag="z_then_late", align_bytes=64)
+        for t in range(4):
+            nc.vector.tensor_scalar(z_bf[:, :, t], ub[t][:], gs_t[:, t : t + 1], None, ALU.mult)
+        z_w = tile("z_w", [P, S], U32)
+        z_s = tile("z_s", [P, S], U8)
+        nc.vector.quantize_mx(out=z_w[:].bitcast(FP8X4), scales=z_s[:], in_=z_bf[:].rearrange("p c t -> p (c t)"))
+
+        late_w = sb.tile([P, H], U32, name="late_w", tag="z_then_late", align_bytes=64)
+        gather_words(late_w[:, 0:HH], d_w, l_k4[:, 16:32])
+        gather_words(late_w[:, HH:], d_w, l_k3[:, 16:32])
+
+        accs = [psum.tile([P, S], F32, name="h2_ps%d" % b) for b in range(4)]
+
+        def pass_k4(b):
+            src = early_w[:, S + b * P : S + (b + 1) * P] if b < 2 else late_w[:, (b - 2) * P : (b - 1) * P]
+            nc.tensor.matmul_mx(
+                out=accs[b][:],
+                lhsT=src.bitcast(FP8X4),
+                lhsT_scale=placed2[:, S + b * P : S + (b + 1) * P],
+                rhs=early_w[:, 0:S].bitcast(FP8X4),
+                rhs_scale=placed2[:, 0:S],
+                start=True,
+                stop=False,
+            )
+
+        def pass_k3(b):
+            src = early_w[:, S + HH + b * P : S + HH + (b + 1) * P] if b < 2 else late_w[:, HH + (b - 2) * P : HH + (b - 1) * P]
+            nc.tensor.matmul_mx(
+                out=accs[b][:],
+                lhsT=src.bitcast(FP8X4),
+                lhsT_scale=placed2[:, S + H + b * P : S + H + (b + 1) * P],
+                rhs=z_w[:].bitcast(FP8X4),
+                rhs_scale=z_s[:],
+                start=False,
+                stop=True,
+            )
+
+        for pair in range(2):
+            for b in (2 * pair, 2 * pair + 1):
+                pass_k4(b)
+            for b in (2 * pair, 2 * pair + 1):
+                pass_k3(b)
+
+        for b in range(4):
+            h2 = tile("h2_%d" % b, [P, S], F32)
+            if b == 0:
+                nc.scalar.activation(h2[:], accs[b][:], ACT.Copy, scale=0.0625)
+            else:
+                nc.vector.tensor_scalar(h2[:], accs[b][:], 0.0625, None, ALU.mult)
+            pa2 = tile("pa2_%d" % b, [P, W], F32)
+            pb2 = tile("pb2_%d" % b, [P, W], F32)
+            ra2 = tile("ra2_%d" % b, [P, W], F32)
+            g7 = tile("g7_%d" % b, [P, S], F32)
+            ub2 = tile("ub2_%d" % b, [P, S], F32)
+            res = tile("res_%d" % b, [P, S], F32)
+            nc.scalar.activation(pa2[:], h2[:].indirect(l_n3[:]), ACT.Copy)
+            nc.scalar.activation(pb2[:], h2[:].indirect(l_n4[:]), ACT.Copy)
+            nc.vector.tensor_tensor(ra2[:], pb2[:], pa2[:], ALU.subtract)
+            nc.scalar.activation(ub2[:].indirect(l_n6[:]), pa2[:], ACT.Copy)
+            nc.scalar.activation(g7[:, 0:W], h2[:].indirect(l_n7[:, 0:8]), ACT.Copy)
+            nc.scalar.activation(g7[:, W:], h2[:].indirect(l_n7[:, 8:16]), ACT.Copy)
+            nc.scalar.activation(ub2[:].indirect(l_n5[:]), ra2[:], ACT.Copy)
+            nc.vector.tensor_tensor(res[:], ub2[:], g7[:], ALU.max)
+            nc.sync.dma_start(out[b * P : (b + 1) * P, :], res[:])

@@ -61,6 +61,11 @@ def tile_picked_mhhzmhpolarcphw_none_p_kernel(
         l_n6 = load_list("l_n6", n6)
         l_n5 = load_list("l_n5", n5)
 
+        warm_in = tile("warm_in", [P, 1], F32)
+        warm_out = tile("warm_out", [P, 1], F32)
+        nc.vector.memset(warm_in[:], 1.0)
+        nc.scalar.activation(warm_out[:], warm_in[:], ACT.Sqrt)
+
         def gather_bytes(dst, table, lst):
             nc.vector.tensor_copy(dst, table[:].indirect(lst))
 

@@ -1,6 +1,7 @@
 from contextlib import ExitStack
 
 import concourse.mybir as mybir
+from concourse.masks import make_identity
 
 K, T, S, G, H, W = 512, 1024, 256, 2048, 512, 128
 P = 128
@@ -74,12 +75,12 @@ def tile_picked_mhhzmhpolarcphw_none_p_kernel(
 
         def place_scale_rows(name, picked, cols, queue):
             placed = tile(name, [P, cols], U8)
-            nc.gpsimd.memset(placed[:].bitcast(I32), 0)
+            nc.vector.memset(placed[:].bitcast(I32), 0)
             for i in range(4):
                 queue.dma_start(placed[i:P:32, :].bitcast(I32), picked[8 * i : P : 32, :].bitcast(I32))
             return placed
 
-        picked1 = tile("picked1", [P, 2 * S + 2 * H], U8)
+        picked1 = sb.tile([P, 2 * S + 2 * H], U8, name="picked1", tag="picked", align_bytes=64)
         gather_bytes(picked1[:, 0:S], x_sc, l_offs[:])
         gather_bytes(picked1[:, S : 2 * S], x_sc, l_hz[:])
         gather_bytes(picked1[:, 2 * S : 2 * S + H], d_sc, l_k1[:])
@@ -88,34 +89,60 @@ def tile_picked_mhhzmhpolarcphw_none_p_kernel(
 
         xq_w = tile("xq_w", [P, S], U32)
         xz_w = tile("xz_w", [P, S], U32)
-        d12_w = tile("d12_w", [P, 2 * H], U32)
+        HH = H // 2
         gather_words(xq_w[:], x_w, l_offs[:])
         gather_words(xz_w[:], x_w, l_hz[:])
-        gather_words(d12_w[:, 0:H], d_w, l_k1[:])
-        gather_words(d12_w[:, H:], d_w, l_k2[:])
+        d1_w = tile("d1_w", [P, H], U32)
+        d2_w = [tile("d2_w%d" % u, [P, HH], U32) for u in range(2)]
+        gather_words(d1_w[:], d_w, l_k1[:])
+        for u in range(2):
+            gather_words(d2_w[u][:], d_w, l_k2[:, 16 * u : 16 * (u + 1)])
 
+        picked2 = sb.tile([P, S + 2 * H], U8, name="picked2", tag="picked", align_bytes=64)
+        gather_bytes(picked2[:, 0:S], x_sc, l_hy[:])
+        gather_bytes(picked2[:, S : S + H], d_sc, l_k4[:])
+        gather_bytes(picked2[:, S + H :], d_sc, l_k3[:])
+        placed2 = place_scale_rows("placed2", picked2, S + 2 * H, nc.sync)
+
+        ident = tile("ident", [P, P], F32)
+        make_identity(nc, ident[:])
+
+        ht_ps = [[psum.tile([P, HH], F32, name="ht_ps%d%d" % (u, c), tag="bank%d" % (2 * u + c)) for c in range(2)] for u in range(2)]
+
+        def ht_pass(j, u, c):
+            xw = (xq_w, xz_w)[j]
+            dw = d1_w[:, u * HH : (u + 1) * HH] if j == 0 else d2_w[u][:]
+            first = 2 * S + j * H + u * HH
+            nc.tensor.matmul_mx(
+                out=ht_ps[u][c][:],
+                lhsT=xw[:, c * P : (c + 1) * P].bitcast(FP8X4),
+                lhsT_scale=placed1[:, j * S + c * P : j * S + (c + 1) * P],
+                rhs=dw.bitcast(FP8X4),
+                rhs_scale=placed1[:, first : first + HH],
+                start=(j == 0),
+                stop=(j == 1),
+            )
+
+        for j in range(2):
+            for u in range(2):
+                for c in range(2):
+                    ht_pass(j, u, c)
+        ht = [tile("ht%d" % c, [P, 4, P], F32) for c in range(2)]
+        for u in range(2):
+            for c in range(2):
+                dst = ht[c][:, :, u * 64 : (u + 1) * 64]
+                src = ht_ps[u][c][:].rearrange("j (m t) -> j t m", t=4)
+                nc.scalar.activation(dst, src, ACT.Copy, scale=0.0625)
         h_sb = []
         for t in range(4):
-            dw = tile("dealt_w%d" % t, [P, 2 * P], I32)
-            ds = tile("dealt_s%d" % t, [P, 2 * P], U8)
-            nc.vector.tensor_copy(dw[:], d12_w[:, t : 2 * H : 4].bitcast(I32))
-            nc.vector.tensor_copy(ds[:], placed1[:, 2 * S + t : 2 * S + 2 * H : 4])
             acc = psum.tile([P, S], F32, name="h_ps%d" % t)
-            for j, xw in enumerate((xq_w, xz_w)):
-                nc.tensor.matmul_mx(
-                    out=acc[:],
-                    lhsT=dw[:, j * P : (j + 1) * P].bitcast(FP8X4),
-                    lhsT_scale=ds[:, j * P : (j + 1) * P],
-                    rhs=xw[:].bitcast(FP8X4),
-                    rhs_scale=placed1[:, j * S : (j + 1) * S],
-                    start=(j == 0),
-                    stop=(j == 1),
-                )
+            for c in range(2):
+                nc.tensor.transpose(acc[:, c * P : (c + 1) * P], ht[c][:, t, :], ident[:])
             h = tile("h%d" % t, [P, S], F32)
             if t == 0:
-                nc.scalar.activation(h[:], acc[:], ACT.Copy, scale=0.0625)
+                nc.scalar.copy(h[:], acc[:])
             else:
-                nc.vector.tensor_scalar(h[:], acc[:], 0.0625, None, ALU.mult)
+                nc.vector.tensor_copy(h[:], acc[:])
             h_sb.append(h)
 
         pab = [tile("pab%d" % u, [P, 2, 2 * W], F32) for u in range(2)]
@@ -127,8 +154,7 @@ def tile_picked_mhhzmhpolarcphw_none_p_kernel(
         ra = tile("ra", [P, 4 * W], F32)
         for u in range(2):
             nc.vector.scalar_tensor_tensor(rb[u][:], pab[u][:, :, 0:W], -0.5, pab[u][:, :, W:], ALU.mult, ALU.add)
-        for u in range(2):
-            sq = sb.tile([P, 2, 2 * W], F32, name="sq%d" % u, tag="scratch%d" % u, align_bytes=64)
+            sq = sb.tile([P, 2, 2 * W], F32, name="sq%d" % u, tag="scratch", align_bytes=64)
             nc.vector.tensor_tensor(sq[:], pab[u][:], pab[u][:], ALU.mult)
             nc.vector.scalar_tensor_tensor(
                 ssq[:, 2 * u * W : 2 * (u + 1) * W].rearrange("p (t w) -> p t w", t=2),
@@ -141,66 +167,65 @@ def tile_picked_mhhzmhpolarcphw_none_p_kernel(
         for t in range(4):
             nc.scalar.activation(ub[t][:].indirect(l_n1[:]), ra[:, t * W : (t + 1) * W], ACT.Copy)
 
-        picked2 = sb.tile([P, S + 2 * H], U8, name="picked2", tag="scratch1", align_bytes=64)
-        gather_bytes(picked2[:, 0:S], x_sc, l_hy[:])
-        gather_bytes(picked2[:, S : S + H], d_sc, l_k4[:])
-        gather_bytes(picked2[:, S + H :], d_sc, l_k3[:])
-        placed2 = place_scale_rows("placed2", picked2, S + 2 * H, nc.sync)
-        HH = H // 2
-        early_w = sb.tile([P, S + H], U32, name="early_w", tag="scratch0", align_bytes=64)
-        gather_words(early_w[:, 0:S], x_w, l_hy[:])
-        gather_words(early_w[:, S : S + HH], d_w, l_k4[:, 0:16])
-        gather_words(early_w[:, S + HH :], d_w, l_k3[:, 0:16])
+        words2 = sb.tile([P, S + 2 * H], U32, name="words2", tag="scratch", align_bytes=64)
+        gather_words(words2[:, 0:S], x_w, l_hy[:])
+        gather_words(words2[:, S : S + H], d_w, l_k4[:])
+        gather_words(words2[:, S + H :], d_w, l_k3[:])
 
-        z_bf = sb.tile([P, S, 4], BF16, name="z_bf", tag="z_then_late", align_bytes=64)
-        for t in range(4):
+        z_bf = tile("z_bf", [P, S, 4], BF16)
+        for t in range(3):
             nc.vector.tensor_scalar(z_bf[:, :, t], ub[t][:], gs_t[:, t : t + 1], None, ALU.mult)
+        for u in range(2):
+            cols = slice(u * W, (u + 1) * W)
+            nc.vector.tensor_scalar(z_bf[:, cols, 3], ub[3][:, cols], gs_t[:, 3:4], None, ALU.mult)
         z_w = tile("z_w", [P, S], U32)
         z_s = tile("z_s", [P, S], U8)
-        nc.vector.quantize_mx(out=z_w[:].bitcast(FP8X4), scales=z_s[:], in_=z_bf[:].rearrange("p c t -> p (c t)"))
+        for u in range(2):
+            cols = slice(u * W, (u + 1) * W)
+            nc.vector.quantize_mx(
+                out=z_w[:, cols].bitcast(FP8X4), scales=z_s[:, cols], in_=z_bf[:, cols, :].rearrange("p c t -> p (c t)")
+            )
 
-        late_w = sb.tile([P, H], U32, name="late_w", tag="z_then_late", align_bytes=64)
-        gather_words(late_w[:, 0:HH], d_w, l_k4[:, 16:32])
-        gather_words(late_w[:, HH:], d_w, l_k3[:, 16:32])
-
-        accs = [psum.tile([P, S], F32, name="h2_ps%d" % b) for b in range(4)]
+        accs = [psum.tile([P, S], F32, name="h2_ps%d" % b, tag="bank%d" % b) for b in range(4)]
 
         def pass_k4(b):
-            src = early_w[:, S + b * P : S + (b + 1) * P] if b < 2 else late_w[:, (b - 2) * P : (b - 1) * P]
+            src = words2[:, S + b * P : S + (b + 1) * P]
             nc.tensor.matmul_mx(
                 out=accs[b][:],
                 lhsT=src.bitcast(FP8X4),
                 lhsT_scale=placed2[:, S + b * P : S + (b + 1) * P],
-                rhs=early_w[:, 0:S].bitcast(FP8X4),
+                rhs=words2[:, 0:S].bitcast(FP8X4),
                 rhs_scale=placed2[:, 0:S],
                 start=True,
                 stop=False,
             )
 
         def pass_k3(b):
-            src = early_w[:, S + HH + b * P : S + HH + (b + 1) * P] if b < 2 else late_w[:, HH + (b - 2) * P : HH + (b - 1) * P]
-            nc.tensor.matmul_mx(
-                out=accs[b][:],
-                lhsT=src.bitcast(FP8X4),
-                lhsT_scale=placed2[:, S + H + b * P : S + H + (b + 1) * P],
-                rhs=z_w[:].bitcast(FP8X4),
-                rhs_scale=z_s[:],
-                start=False,
-                stop=True,
-            )
-
-        for pair in range(2):
-            for b in (2 * pair, 2 * pair + 1):
-                pass_k4(b)
-            for b in (2 * pair, 2 * pair + 1):
-                pass_k3(b)
+            src = words2[:, S + H + b * P : S + H + (b + 1) * P]
+            parts = (slice(0, W), slice(W, S)) if b == 0 else (slice(0, S),)
+            for cols in parts:
+                nc.tensor.matmul_mx(
+                    out=accs[b][:, cols],
+                    lhsT=src.bitcast(FP8X4),
+                    lhsT_scale=placed2[:, S + H + b * P : S + H + (b + 1) * P],
+                    rhs=z_w[:, cols].bitcast(FP8X4),
+                    rhs_scale=z_s[:, cols],
+                    start=False,
+                    stop=(cols.stop == S),
+                )
 
         for b in range(4):
-            h2 = tile("h2_%d" % b, [P, S], F32)
+            pass_k4(b)
+        for b in range(4):
+            pass_k3(b)
+
+        for b in range(4):
+            h2 = tile("h2_%d" % b, [P, S + 8], F32)
+            nc.vector.memset(h2[:, S:], 0.0)
             if b == 0:
-                nc.scalar.activation(h2[:], accs[b][:], ACT.Copy, scale=0.0625)
+                nc.scalar.activation(h2[:, 0:S], accs[b][:], ACT.Copy, scale=0.0625)
             else:
-                nc.vector.tensor_scalar(h2[:], accs[b][:], 0.0625, None, ALU.mult)
+                nc.vector.tensor_scalar(h2[:, 0:S], accs[b][:], 0.0625, None, ALU.mult)
             pa2 = tile("pa2_%d" % b, [P, W], F32)
             pb2 = tile("pb2_%d" % b, [P, W], F32)
             ra2 = tile("ra2_%d" % b, [P, W], F32)
@@ -211,8 +236,7 @@ def tile_picked_mhhzmhpolarcphw_none_p_kernel(
             nc.scalar.activation(pb2[:], h2[:].indirect(l_n4[:]), ACT.Copy)
             nc.vector.tensor_tensor(ra2[:], pb2[:], pa2[:], ALU.subtract)
             nc.scalar.activation(ub2[:].indirect(l_n6[:]), pa2[:], ACT.Copy)
-            nc.scalar.activation(g7[:, 0:W], h2[:].indirect(l_n7[:, 0:8]), ACT.Copy)
-            nc.scalar.activation(g7[:, W:], h2[:].indirect(l_n7[:, 8:16]), ACT.Copy)
+            nc.scalar.activation(g7[:], h2[:].indirect(l_n7[:]), ACT.Copy)
             nc.scalar.activation(ub2[:].indirect(l_n5[:]), ra2[:], ACT.Copy)
             nc.vector.tensor_tensor(res[:], ub2[:], g7[:], ALU.max)
             nc.sync.dma_start(out[b * P : (b + 1) * P, :], res[:])

@@ -5,6 +5,12 @@ from concourse.masks import make_identity
 
 K, T, S, G, H, W = 512, 1024, 256, 2048, 512, 128
 P = 128
+PACK = 4
+SCALE_ROWS = K // 32
+HALF = H // 2
+HALF_COLS = HALF // 16
+SPARE = 8
+SIXTEENTH = 0.0625
 FLOPS = 4 * 2 * K * H * S
 
 F32, BF16 = mybir.dt.float32, mybir.dt.bfloat16
@@ -22,24 +28,24 @@ def tile_picked_mhhzmhpolarcphw_none_p_kernel(
         sb = ctx.enter_context(tc.tile_pool(name="sb", bufs=1))
         psum = ctx.enter_context(tc.psum_pool(name="psum", bufs=1))
 
-        def tile(name, shape, dtype):
-            return sb.tile(shape, dtype, name=name, align_bytes=64)
+        def tile(name, shape, dtype, tag=None):
+            return sb.tile(shape, dtype, name=name, tag=tag or name, align_bytes=64)
 
         def load_list(name, src):
-            t = tile(name, list(src.shape), U16)
-            nc.sync.dma_start(t[:], src)
-            return t
+            lst = tile(name, list(src.shape), U16)
+            nc.sync.dma_start(lst[:], src)
+            return lst
 
         def load_scale_table(name, src, cols):
-            t = tile(name, [P, cols], U8)
-            rows = src[0].bitcast(I32).unsqueeze(1).broadcast_to([16, 8, cols // 4])
-            nc.sync.dma_start(t[:].bitcast(I32), rows)
-            return t
+            table = tile(name, [P, cols], U8)
+            rows = src[0].bitcast(I32).unsqueeze(1).broadcast_to([SCALE_ROWS, P // SCALE_ROWS, cols // 4])
+            nc.sync.dma_start(table[:].bitcast(I32), rows)
+            return table
 
         def load_word_table(name, src, cols):
-            t = tile(name, [P, cols], I32)
-            nc.sync.dma_start(t[:], src[0].rearrange("p n t -> p (n t)").bitcast(I32))
-            return t
+            table = tile(name, [P, cols], I32)
+            nc.sync.dma_start(table[:], src[0].rearrange("p n t -> p (n t)").bitcast(I32))
+            return table
 
         x_sc = load_scale_table("x_sc", x_scales, T)
         l_offs = load_list("l_offs", offs)
@@ -51,8 +57,8 @@ def tile_picked_mhhzmhpolarcphw_none_p_kernel(
         d_w = load_word_table("d_w", d_words, G)
         l_n1 = load_list("l_n1", n1)
         l_n2 = load_list("l_n2", n2)
-        gs_t = tile("gs_t", [P, 4], F32)
-        nc.sync.dma_start(gs_t[:], gs.rearrange("(p t) o -> p (t o)", t=4))
+        gs_t = tile("gs_t", [P, PACK], F32)
+        nc.sync.dma_start(gs_t[:], gs.rearrange("(p t) o -> p (t o)", t=PACK))
         l_hy = load_list("l_hy", hy)
         l_k4 = load_list("l_k4", k4)
         l_k3 = load_list("l_k3", k3)
@@ -80,7 +86,13 @@ def tile_picked_mhhzmhpolarcphw_none_p_kernel(
                 queue.dma_start(placed[i:P:32, :].bitcast(I32), picked[8 * i : P : 32, :].bitcast(I32))
             return placed
 
-        picked1 = sb.tile([P, 2 * S + 2 * H], U8, name="picked1", tag="picked", align_bytes=64)
+        def fetch(dst, window, lst):
+            nc.scalar.activation(dst, window[:].indirect(lst[:]), ACT.Copy)
+
+        def put(window, lst, src):
+            nc.scalar.activation(window[:].indirect(lst[:]), src, ACT.Copy)
+
+        picked1 = tile("picked1", [P, 2 * S + 2 * H], U8, tag="picked")
         gather_bytes(picked1[:, 0:S], x_sc, l_offs[:])
         gather_bytes(picked1[:, S : 2 * S], x_sc, l_hz[:])
         gather_bytes(picked1[:, 2 * S : 2 * S + H], d_sc, l_k1[:])
@@ -89,16 +101,15 @@ def tile_picked_mhhzmhpolarcphw_none_p_kernel(
 
         xq_w = tile("xq_w", [P, S], U32)
         xz_w = tile("xz_w", [P, S], U32)
-        HH = H // 2
         gather_words(xq_w[:], x_w, l_offs[:])
         gather_words(xz_w[:], x_w, l_hz[:])
         d1_w = tile("d1_w", [P, H], U32)
-        d2_w = [tile("d2_w%d" % u, [P, HH], U32) for u in range(2)]
+        d2_w = [tile("d2_w%d" % u, [P, HALF], U32) for u in range(2)]
         gather_words(d1_w[:], d_w, l_k1[:])
         for u in range(2):
-            gather_words(d2_w[u][:], d_w, l_k2[:, 16 * u : 16 * (u + 1)])
+            gather_words(d2_w[u][:], d_w, l_k2[:, HALF_COLS * u : HALF_COLS * (u + 1)])
 
-        picked2 = sb.tile([P, S + 2 * H], U8, name="picked2", tag="picked", align_bytes=64)
+        picked2 = tile("picked2", [P, S + 2 * H], U8, tag="picked")
         gather_bytes(picked2[:, 0:S], x_sc, l_hy[:])
         gather_bytes(picked2[:, S : S + H], d_sc, l_k4[:])
         gather_bytes(picked2[:, S + H :], d_sc, l_k3[:])
@@ -107,136 +118,119 @@ def tile_picked_mhhzmhpolarcphw_none_p_kernel(
         ident = tile("ident", [P, P], F32)
         make_identity(nc, ident[:])
 
-        ht_ps = [[psum.tile([P, HH], F32, name="ht_ps%d%d" % (u, c), tag="bank%d" % (2 * u + c)) for c in range(2)] for u in range(2)]
-
-        def ht_pass(j, u, c):
-            xw = (xq_w, xz_w)[j]
-            dw = d1_w[:, u * HH : (u + 1) * HH] if j == 0 else d2_w[u][:]
-            first = 2 * S + j * H + u * HH
-            nc.tensor.matmul_mx(
-                out=ht_ps[u][c][:],
-                lhsT=xw[:, c * P : (c + 1) * P].bitcast(FP8X4),
-                lhsT_scale=placed1[:, j * S + c * P : j * S + (c + 1) * P],
-                rhs=dw.bitcast(FP8X4),
-                rhs_scale=placed1[:, first : first + HH],
-                start=(j == 0),
-                stop=(j == 1),
-            )
-
-        for j in range(2):
+        ht_ps = [psum.tile([P, 2, HALF], F32, name="ht_ps%d" % u, tag="bank%d" % (u + 1)) for u in range(2)]
+        for term, xw in enumerate((xq_w, xz_w)):
             for u in range(2):
+                dw = d1_w[:, u * HALF : (u + 1) * HALF] if term == 0 else d2_w[u][:]
+                first = 2 * S + term * H + u * HALF
                 for c in range(2):
-                    ht_pass(j, u, c)
-        ht = [tile("ht%d" % c, [P, 4, P], F32) for c in range(2)]
+                    nc.tensor.matmul_mx(
+                        out=ht_ps[u][:, c, :],
+                        lhsT=xw[:, c * P : (c + 1) * P].bitcast(FP8X4),
+                        lhsT_scale=placed1[:, term * S + c * P : term * S + (c + 1) * P],
+                        rhs=dw.bitcast(FP8X4),
+                        rhs_scale=placed1[:, first : first + HALF],
+                        start=(term == 0 and c == 0),
+                        stop=(term == 1 and c == 1),
+                    )
+        ht_first = tile("ht_first", [P, 2, P], F32)
+        ht_rest = tile("ht_rest", [P, 2, PACK - 1, P], F32)
         for u in range(2):
+            ps = slice(u * HALF // PACK, (u + 1) * HALF // PACK)
+            src = ht_ps[u][:].rearrange("j c (m t) -> j c t m", t=PACK)
+            nc.scalar.activation(ht_first[:, :, ps], src[:, :, 0, :], ACT.Copy, scale=SIXTEENTH)
+            nc.scalar.activation(ht_rest[:, :, :, ps], src[:, :, 1:PACK, :], ACT.Copy, scale=SIXTEENTH)
+        h = []
+        for t in range(PACK):
+            turned = psum.tile([P, S], F32, name="h_ps%d" % t, tag="bank%d" % (t + 3))
             for c in range(2):
-                dst = ht[c][:, :, u * 64 : (u + 1) * 64]
-                src = ht_ps[u][c][:].rearrange("j (m t) -> j t m", t=4)
-                nc.scalar.activation(dst, src, ACT.Copy, scale=0.0625)
-        h_sb = []
-        for t in range(4):
-            acc = psum.tile([P, S], F32, name="h_ps%d" % t)
-            for c in range(2):
-                nc.tensor.transpose(acc[:, c * P : (c + 1) * P], ht[c][:, t, :], ident[:])
-            h = tile("h%d" % t, [P, S], F32)
+                block = ht_first[:, c, :] if t == 0 else ht_rest[:, c, t - 1, :]
+                nc.tensor.transpose(turned[:, c * P : (c + 1) * P], block, ident[:])
+            h.append(tile("h%d" % t, [P, S], F32))
             if t == 0:
-                nc.scalar.copy(h[:], acc[:])
+                nc.scalar.copy(h[t][:], turned[:])
             else:
-                nc.vector.tensor_copy(h[:], acc[:])
-            h_sb.append(h)
+                nc.vector.tensor_copy(h[t][:], turned[:])
 
-        pab = [tile("pab%d" % u, [P, 2, 2 * W], F32) for u in range(2)]
-        for t in range(4):
-            nc.scalar.activation(pab[t // 2][:, t % 2, 0:W], h_sb[t][:].indirect(l_n1[:]), ACT.Copy)
-            nc.scalar.activation(pab[t // 2][:, t % 2, W:], h_sb[t][:].indirect(l_n2[:]), ACT.Copy)
-        rb = [tile("rb%d" % u, [P, 2, W], F32) for u in range(2)]
-        ssq = tile("ssq", [P, 4 * W], F32)
-        ra = tile("ra", [P, 4 * W], F32)
-        for u in range(2):
-            nc.vector.scalar_tensor_tensor(rb[u][:], pab[u][:, :, 0:W], -0.5, pab[u][:, :, W:], ALU.mult, ALU.add)
-            sq = sb.tile([P, 2, 2 * W], F32, name="sq%d" % u, tag="scratch", align_bytes=64)
-            nc.vector.tensor_tensor(sq[:], pab[u][:], pab[u][:], ALU.mult)
+        pab = [tile("pab%d" % pair, [P, 2, 2 * W], F32) for pair in range(2)]
+        for t in range(PACK):
+            fetch(pab[t // 2][:, t % 2, 0:W], h[t], l_n1)
+            fetch(pab[t // 2][:, t % 2, W:], h[t], l_n2)
+        rb = [tile("rb%d" % pair, [P, 2, W], F32) for pair in range(2)]
+        radicand = tile("radicand", [P, PACK * W], F32)
+        ra = tile("ra", [P, PACK * W], F32)
+        for pair in range(2):
+            nc.vector.scalar_tensor_tensor(rb[pair][:], pab[pair][:, :, 0:W], -0.5, pab[pair][:, :, W:], ALU.mult, ALU.add)
+            squares = tile("squares%d" % pair, [P, 2, 2 * W], F32, tag="scratch")
+            nc.vector.tensor_tensor(squares[:], pab[pair][:], pab[pair][:], ALU.mult)
             nc.vector.scalar_tensor_tensor(
-                ssq[:, 2 * u * W : 2 * (u + 1) * W].rearrange("p (t w) -> p t w", t=2),
-                sq[:, :, 0:W], 0.25, sq[:, :, W:], ALU.add, ALU.add,
+                radicand[:, 2 * pair * W : 2 * (pair + 1) * W].rearrange("p (t w) -> p t w", t=2),
+                squares[:, :, 0:W],
+                0.25,
+                squares[:, :, W:],
+                ALU.add,
+                ALU.add,
             )
-        ub = [tile("ub%d" % t, [P, S], F32) for t in range(4)]
-        for t in range(4):
-            nc.scalar.activation(ub[t][:].indirect(l_n2[:]), rb[t // 2][:, t % 2, :], ACT.Copy)
-        nc.scalar.activation(ra[:], ssq[:], ACT.Sqrt)
-        for t in range(4):
-            nc.scalar.activation(ub[t][:].indirect(l_n1[:]), ra[:, t * W : (t + 1) * W], ACT.Copy)
+        ub = [tile("ub%d" % t, [P, S], F32) for t in range(PACK)]
+        for t in range(PACK):
+            put(ub[t], l_n2, rb[t // 2][:, t % 2, :])
+        nc.scalar.activation(ra[:], radicand[:], ACT.Sqrt)
+        for t in range(PACK):
+            put(ub[t], l_n1, ra[:, t * W : (t + 1) * W])
 
-        words2 = sb.tile([P, S + 2 * H], U32, name="words2", tag="scratch", align_bytes=64)
+        words2 = tile("words2", [P, S + 2 * H], U32, tag="scratch")
         gather_words(words2[:, 0:S], x_w, l_hy[:])
         gather_words(words2[:, S : S + H], d_w, l_k4[:])
         gather_words(words2[:, S + H :], d_w, l_k3[:])
 
-        z_bf = tile("z_bf", [P, S, 4], BF16)
-        for t in range(3):
+        halves = (slice(0, S // 2), slice(S // 2, S))
+        last = PACK - 1
+        z_bf = tile("z_bf", [P, S, PACK], BF16)
+        for t in range(last):
             nc.vector.tensor_scalar(z_bf[:, :, t], ub[t][:], gs_t[:, t : t + 1], None, ALU.mult)
-        for u in range(2):
-            cols = slice(u * W, (u + 1) * W)
-            nc.vector.tensor_scalar(z_bf[:, cols, 3], ub[3][:, cols], gs_t[:, 3:4], None, ALU.mult)
+        for cols in halves:
+            nc.vector.tensor_scalar(z_bf[:, cols, last], ub[last][:, cols], gs_t[:, last:], None, ALU.mult)
         z_w = tile("z_w", [P, S], U32)
         z_s = tile("z_s", [P, S], U8)
-        for u in range(2):
-            cols = slice(u * W, (u + 1) * W)
+        for cols in halves:
             nc.vector.quantize_mx(
                 out=z_w[:, cols].bitcast(FP8X4), scales=z_s[:, cols], in_=z_bf[:, cols, :].rearrange("p c t -> p (c t)")
             )
 
-        accs = [psum.tile([P, S], F32, name="h2_ps%d" % b, tag="bank%d" % b) for b in range(4)]
-
-        def pass_k4(b):
-            src = words2[:, S + b * P : S + (b + 1) * P]
-            nc.tensor.matmul_mx(
-                out=accs[b][:],
-                lhsT=src.bitcast(FP8X4),
-                lhsT_scale=placed2[:, S + b * P : S + (b + 1) * P],
-                rhs=words2[:, 0:S].bitcast(FP8X4),
-                rhs_scale=placed2[:, 0:S],
-                start=True,
-                stop=False,
-            )
-
-        def pass_k3(b):
-            src = words2[:, S + H + b * P : S + H + (b + 1) * P]
-            parts = (slice(0, W), slice(W, S)) if b == 0 else (slice(0, S),)
-            for cols in parts:
+        pieces = [(0, halves[0], "bank0"), (0, halves[1], "bank7")] + [(b, slice(0, S), "bank%d" % b) for b in (1, 2, 3)]
+        sums = [psum.tile([P, cols.stop - cols.start], F32, name="h2_ps%d" % i, tag=bank) for i, (b, cols, bank) in enumerate(pieces)]
+        for term, (rhs, rhs_scale) in enumerate(((words2, placed2), (z_w, z_s))):
+            for acc, (b, cols, bank) in zip(sums, pieces):
+                codes = slice(S + term * H + b * P, S + term * H + (b + 1) * P)
                 nc.tensor.matmul_mx(
-                    out=accs[b][:, cols],
-                    lhsT=src.bitcast(FP8X4),
-                    lhsT_scale=placed2[:, S + H + b * P : S + H + (b + 1) * P],
-                    rhs=z_w[:, cols].bitcast(FP8X4),
-                    rhs_scale=z_s[:, cols],
-                    start=False,
-                    stop=(cols.stop == S),
+                    out=acc[:],
+                    lhsT=words2[:, codes].bitcast(FP8X4),
+                    lhsT_scale=placed2[:, codes],
+                    rhs=rhs[:, cols].bitcast(FP8X4),
+                    rhs_scale=rhs_scale[:, cols],
+                    start=(term == 0),
+                    stop=(term == 1),
                 )
 
-        for b in range(4):
-            pass_k4(b)
-        for b in range(4):
-            pass_k3(b)
-
-        for b in range(4):
-            h2 = tile("h2_%d" % b, [P, S + 8], F32)
+        for b in range(H // P):
+            h2 = tile("h2_%d" % b, [P, S + SPARE], F32)
             nc.vector.memset(h2[:, S:], 0.0)
             if b == 0:
-                nc.scalar.activation(h2[:, 0:S], accs[b][:], ACT.Copy, scale=0.0625)
+                for acc, cols in zip(sums, halves):
+                    nc.scalar.activation(h2[:, cols], acc[:], ACT.Copy, scale=SIXTEENTH)
             else:
-                nc.vector.tensor_scalar(h2[:, 0:S], accs[b][:], 0.0625, None, ALU.mult)
+                nc.vector.tensor_scalar(h2[:, 0:S], sums[b + 1][:], SIXTEENTH, None, ALU.mult)
             pa2 = tile("pa2_%d" % b, [P, W], F32)
             pb2 = tile("pb2_%d" % b, [P, W], F32)
             ra2 = tile("ra2_%d" % b, [P, W], F32)
-            g7 = tile("g7_%d" % b, [P, S], F32)
+            h2_n7 = tile("h2_n7_%d" % b, [P, S], F32)
             ub2 = tile("ub2_%d" % b, [P, S], F32)
             res = tile("res_%d" % b, [P, S], F32)
-            nc.scalar.activation(pa2[:], h2[:].indirect(l_n3[:]), ACT.Copy)
-            nc.scalar.activation(pb2[:], h2[:].indirect(l_n4[:]), ACT.Copy)
+            fetch(pa2[:], h2, l_n3)
+            fetch(pb2[:], h2, l_n4)
             nc.vector.tensor_tensor(ra2[:], pb2[:], pa2[:], ALU.subtract)
-            nc.scalar.activation(ub2[:].indirect(l_n6[:]), pa2[:], ACT.Copy)
-            nc.scalar.activation(g7[:], h2[:].indirect(l_n7[:]), ACT.Copy)
-            nc.scalar.activation(ub2[:].indirect(l_n5[:]), ra2[:], ACT.Copy)
-            nc.vector.tensor_tensor(res[:], ub2[:], g7[:], ALU.max)
+            put(ub2, l_n6, pa2[:])
+            fetch(h2_n7[:], h2, l_n7)
+            put(ub2, l_n5, ra2[:])
+            nc.vector.tensor_tensor(res[:], ub2[:], h2_n7[:], ALU.max)
             nc.sync.dma_start(out[b * P : (b + 1) * P, :], res[:])

@@ -147,7 +147,7 @@ def tile_picked_mhhzmhpolarcphw_none_p_kernel(
                 block = ht_first[:, c, :] if t == 0 else ht_rest[:, c, t - 1, :]
                 nc.tensor.transpose(turned[:, c * P : (c + 1) * P], block, ident[:])
             h.append(tile("h%d" % t, [P, S], F32))
-            if t == 0:
+            if t < 2:
                 nc.scalar.copy(h[t][:], turned[:])
             else:
                 nc.vector.tensor_copy(h[t][:], turned[:])

from contextlib import ExitStack

import concourse.mybir as mybir
from concourse.masks import make_identity

K, T, S, G, H, W = 512, 1024, 256, 2048, 512, 128
P = 128
PACK = 4
SCALE_ROWS = K // 32
HALF = H // 2
HALF_COLS = HALF // 16
SPARE = 8
SIXTEENTH = 0.0625
FLOPS = 4 * 2 * K * H * S

F32, BF16 = mybir.dt.float32, mybir.dt.bfloat16
I32, U32, U16, U8 = mybir.dt.int32, mybir.dt.uint32, mybir.dt.uint16, mybir.dt.uint8
FP8X4 = mybir.dt.float8_e4m3fn_x4
ALU = mybir.AluOpType
ACT = mybir.ActivationFunctionType


def tile_picked_mhhzmhpolarcphw_none_p_kernel(
    tc, x_words, x_scales, d_words, d_scales, gs, offs, k1, hz, k2, n1, n2, k3, k4, hy, n3, n4, n5, n6, n7, out
):
    nc = tc.nc
    with ExitStack() as ctx:
        sb = ctx.enter_context(tc.tile_pool(name="sb", bufs=1))
        psum = ctx.enter_context(tc.psum_pool(name="psum", bufs=1))

        def tile(name, shape, dtype, tag=None):
            return sb.tile(shape, dtype, name=name, tag=tag or name, align_bytes=64)

        def load_list(name, src):
            lst = tile(name, list(src.shape), U16)
            nc.sync.dma_start(lst[:], src)
            return lst

        def load_scale_table(name, src, cols):
            table = tile(name, [P, cols], U8)
            rows = src[0].bitcast(I32).unsqueeze(1).broadcast_to([SCALE_ROWS, P // SCALE_ROWS, cols // 4])
            nc.sync.dma_start(table[:].bitcast(I32), rows)
            return table

        def load_word_table(name, src, cols):
            table = tile(name, [P, cols], I32)
            nc.sync.dma_start(table[:], src[0].rearrange("p n t -> p (n t)").bitcast(I32))
            return table

        x_sc = load_scale_table("x_sc", x_scales, T)
        l_offs = load_list("l_offs", offs)
        d_sc = load_scale_table("d_sc", d_scales, G)
        l_hz = load_list("l_hz", hz)
        l_k1 = load_list("l_k1", k1)
        l_k2 = load_list("l_k2", k2)
        x_w = load_word_table("x_w", x_words, T)
        d_w = load_word_table("d_w", d_words, G)
        l_n1 = load_list("l_n1", n1)
        l_n2 = load_list("l_n2", n2)
        gs_t = tile("gs_t", [P, PACK], F32)
        nc.sync.dma_start(gs_t[:], gs.rearrange("(p t) o -> p (t o)", t=PACK))
        l_hy = load_list("l_hy", hy)
        l_k4 = load_list("l_k4", k4)
        l_k3 = load_list("l_k3", k3)
        l_n3 = load_list("l_n3", n3)
        l_n4 = load_list("l_n4", n4)
        l_n7 = load_list("l_n7", n7)
        l_n6 = load_list("l_n6", n6)
        l_n5 = load_list("l_n5", n5)

        warm_in = tile("warm_in", [P, 1], F32)
        warm_out = tile("warm_out", [P, 1], F32)
        nc.vector.memset(warm_in[:], 1.0)
        nc.scalar.activation(warm_out[:], warm_in[:], ACT.Sqrt)

        def gather_bytes(dst, table, lst):
            nc.vector.tensor_copy(dst, table[:].indirect(lst))

        def gather_words(dst, table, lst):
            nc.vector.tensor_copy(dst, table[:].bitcast(U32).indirect(lst))

        def place_scale_rows(name, picked, cols, queue):
            placed = tile(name, [P, cols], U8)
            nc.vector.memset(placed[:].bitcast(I32), 0)
            for i in range(4):
                queue.dma_start(placed[i:P:32, :].bitcast(I32), picked[8 * i : P : 32, :].bitcast(I32))
            return placed

        def fetch(dst, window, lst):
            nc.scalar.activation(dst, window[:].indirect(lst[:]), ACT.Copy)

        def put(window, lst, src):
            nc.scalar.activation(window[:].indirect(lst[:]), src, ACT.Copy)

        picked1 = tile("picked1", [P, 2 * S + 2 * H], U8, tag="picked")
        gather_bytes(picked1[:, 0:S], x_sc, l_offs[:])
        gather_bytes(picked1[:, S : 2 * S], x_sc, l_hz[:])
        gather_bytes(picked1[:, 2 * S : 2 * S + H], d_sc, l_k1[:])
        gather_bytes(picked1[:, 2 * S + H :], d_sc, l_k2[:])
        placed1 = place_scale_rows("placed1", picked1, 2 * S + 2 * H, nc.scalar)

        xq_w = tile("xq_w", [P, S], U32)
        xz_w = tile("xz_w", [P, S], U32)
        gather_words(xq_w[:], x_w, l_offs[:])
        gather_words(xz_w[:], x_w, l_hz[:])
        d1_w = tile("d1_w", [P, H], U32)
        d2_w = [tile("d2_w%d" % u, [P, HALF], U32) for u in range(2)]
        gather_words(d1_w[:], d_w, l_k1[:])
        for u in range(2):
            gather_words(d2_w[u][:], d_w, l_k2[:, HALF_COLS * u : HALF_COLS * (u + 1)])

        picked2 = tile("picked2", [P, S + 2 * H], U8, tag="picked")
        gather_bytes(picked2[:, 0:S], x_sc, l_hy[:])
        gather_bytes(picked2[:, S : S + H], d_sc, l_k4[:])
        gather_bytes(picked2[:, S + H :], d_sc, l_k3[:])
        placed2 = place_scale_rows("placed2", picked2, S + 2 * H, nc.sync)

        ident = tile("ident", [P, P], F32)
        make_identity(nc, ident[:])

        ht_ps = [psum.tile([P, 2, HALF], F32, name="ht_ps%d" % u, tag="bank%d" % (u + 1)) for u in range(2)]
        for term, xw in enumerate((xq_w, xz_w)):
            for u in range(2):
                dw = d1_w[:, u * HALF : (u + 1) * HALF] if term == 0 else d2_w[u][:]
                first = 2 * S + term * H + u * HALF
                for c in range(2):
                    nc.tensor.matmul_mx(
                        out=ht_ps[u][:, c, :],
                        lhsT=xw[:, c * P : (c + 1) * P].bitcast(FP8X4),
                        lhsT_scale=placed1[:, term * S + c * P : term * S + (c + 1) * P],
                        rhs=dw.bitcast(FP8X4),
                        rhs_scale=placed1[:, first : first + HALF],
                        start=(term == 0 and c == 0),
                        stop=(term == 1 and c == 1),
                    )
        ht_first = tile("ht_first", [P, 2, P], F32)
        ht_rest = tile("ht_rest", [P, 2, PACK - 1, P], F32)
        for u in range(2):
            ps = slice(u * HALF // PACK, (u + 1) * HALF // PACK)
            src = ht_ps[u][:].rearrange("j c (m t) -> j c t m", t=PACK)
            nc.scalar.activation(ht_first[:, :, ps], src[:, :, 0, :], ACT.Copy, scale=SIXTEENTH)
            nc.scalar.activation(ht_rest[:, :, :, ps], src[:, :, 1:PACK, :], ACT.Copy, scale=SIXTEENTH)
        h = []
        for t in range(PACK):
            turned = psum.tile([P, S], F32, name="h_ps%d" % t, tag="bank%d" % (t + 3))
            for c in range(2):
                block = ht_first[:, c, :] if t == 0 else ht_rest[:, c, t - 1, :]
                nc.tensor.transpose(turned[:, c * P : (c + 1) * P], block, ident[:])
            h.append(tile("h%d" % t, [P, S], F32))
            if t < 2:
                nc.scalar.copy(h[t][:], turned[:])
            else:
                nc.vector.tensor_copy(h[t][:], turned[:])

        pab = [tile("pab%d" % pair, [P, 2, 2 * W], F32) for pair in range(2)]
        for t in range(PACK):
            fetch(pab[t // 2][:, t % 2, 0:W], h[t], l_n1)
            fetch(pab[t // 2][:, t % 2, W:], h[t], l_n2)
        rb = [tile("rb%d" % pair, [P, 2, W], F32) for pair in range(2)]
        radicand = tile("radicand", [P, PACK * W], F32)
        ra = tile("ra", [P, PACK * W], F32)
        for pair in range(2):
            nc.vector.scalar_tensor_tensor(rb[pair][:], pab[pair][:, :, 0:W], -0.5, pab[pair][:, :, W:], ALU.mult, ALU.add)
            squares = tile("squares%d" % pair, [P, 2, 2 * W], F32, tag="scratch")
            nc.vector.tensor_tensor(squares[:], pab[pair][:], pab[pair][:], ALU.mult)
            nc.vector.scalar_tensor_tensor(
                radicand[:, 2 * pair * W : 2 * (pair + 1) * W].rearrange("p (t w) -> p t w", t=2),
                squares[:, :, 0:W],
                0.25,
                squares[:, :, W:],
                ALU.add,
                ALU.add,
            )
        ub = [tile("ub%d" % t, [P, S], F32) for t in range(PACK)]
        for t in range(PACK):
            put(ub[t], l_n2, rb[t // 2][:, t % 2, :])
        nc.scalar.activation(ra[:], radicand[:], ACT.Sqrt)
        for t in range(PACK):
            put(ub[t], l_n1, ra[:, t * W : (t + 1) * W])

        words2 = tile("words2", [P, S + 2 * H], U32, tag="scratch")
        gather_words(words2[:, 0:S], x_w, l_hy[:])
        gather_words(words2[:, S : S + H], d_w, l_k4[:])
        gather_words(words2[:, S + H :], d_w, l_k3[:])

        halves = (slice(0, S // 2), slice(S // 2, S))
        last = PACK - 1
        z_bf = tile("z_bf", [P, S, PACK], BF16)
        for t in range(last):
            nc.vector.tensor_scalar(z_bf[:, :, t], ub[t][:], gs_t[:, t : t + 1], None, ALU.mult)
        for cols in halves:
            nc.vector.tensor_scalar(z_bf[:, cols, last], ub[last][:, cols], gs_t[:, last:], None, ALU.mult)
        z_w = tile("z_w", [P, S], U32)
        z_s = tile("z_s", [P, S], U8)
        for cols in halves:
            nc.vector.quantize_mx(
                out=z_w[:, cols].bitcast(FP8X4), scales=z_s[:, cols], in_=z_bf[:, cols, :].rearrange("p c t -> p (c t)")
            )

        pieces = [(0, halves[0], "bank0"), (0, halves[1], "bank7")] + [(b, slice(0, S), "bank%d" % b) for b in (1, 2, 3)]
        sums = [psum.tile([P, cols.stop - cols.start], F32, name="h2_ps%d" % i, tag=bank) for i, (b, cols, bank) in enumerate(pieces)]
        for term, (rhs, rhs_scale) in enumerate(((words2, placed2), (z_w, z_s))):
            for acc, (b, cols, bank) in zip(sums, pieces):
                codes = slice(S + term * H + b * P, S + term * H + (b + 1) * P)
                nc.tensor.matmul_mx(
                    out=acc[:],
                    lhsT=words2[:, codes].bitcast(FP8X4),
                    lhsT_scale=placed2[:, codes],
                    rhs=rhs[:, cols].bitcast(FP8X4),
                    rhs_scale=rhs_scale[:, cols],
                    start=(term == 0),
                    stop=(term == 1),
                )

        for b in range(H // P):
            h2 = tile("h2_%d" % b, [P, S + SPARE], F32)
            nc.vector.memset(h2[:, S:], 0.0)
            if b == 0:
                for acc, cols in zip(sums, halves):
                    nc.scalar.activation(h2[:, cols], acc[:], ACT.Copy, scale=SIXTEENTH)
            else:
                nc.vector.tensor_scalar(h2[:, 0:S], sums[b + 1][:], SIXTEENTH, None, ALU.mult)
            pa2 = tile("pa2_%d" % b, [P, W], F32)
            pb2 = tile("pb2_%d" % b, [P, W], F32)
            ra2 = tile("ra2_%d" % b, [P, W], F32)
            h2_n7 = tile("h2_n7_%d" % b, [P, S], F32)
            ub2 = tile("ub2_%d" % b, [P, S], F32)
            res = tile("res_%d" % b, [P, S], F32)
            fetch(pa2[:], h2, l_n3)
            fetch(pb2[:], h2, l_n4)
            nc.vector.tensor_tensor(ra2[:], pb2[:], pa2[:], ALU.subtract)
            put(ub2, l_n6, pa2[:])
            fetch(h2_n7[:], h2, l_n7)
            put(ub2, l_n5, ra2[:])
            nc.vector.tensor_tensor(res[:], ub2[:], h2_n7[:], ALU.max)
            nc.sync.dma_start(out[b * P : (b + 1) * P, :], res[:])
